import numpy as np
import ml_dtypes


def mxq(x, axis, fmt="e4m3"):
    dtype, down = {"e4m3": (ml_dtypes.float8_e4m3fn, 7), "e5m2": (ml_dtypes.float8_e5m2, 14)}[fmt]
    v = np.moveaxis(np.asarray(x, np.float32).astype(ml_dtypes.bfloat16).astype(np.float64), axis, -1)
    blocks = v.reshape(v.shape[:-1] + (-1, 32))
    amax = np.abs(blocks).max(-1, keepdims=True)
    byte = np.maximum(np.where(amax > 0, np.frexp(amax)[1] - 1 + 127, 0) - down, 1)
    scale = np.exp2(byte - 127.0)
    codes = (blocks / scale).astype(np.float32).astype(dtype).astype(np.float64)
    return np.moveaxis((codes * scale).reshape(v.shape), -1, axis)


WIDE = False


def mx_kscale(k):
    if not WIDE:
        return np.ones(k)
    levels = np.array([10, -10, 5, -5, 0])
    if k % 512:
        return np.exp2(np.random.permutation(np.resize(levels, k // 32))).repeat(32)
    a = np.empty((k // 512, 16))
    for p in range(k // 512):
        a[p, :8] = np.random.permutation(np.resize(levels, 8))
        for g in range(8):
            far = levels[np.abs(levels - a[p, g]) >= 10]
            a[p, g + 8] = far[np.random.randint(len(far))]
    return np.exp2(a.ravel()).repeat(32)


def f64(x):
    return np.asarray(x).astype(np.float64)


def striped(idx):
    return np.tile(idx.reshape(-1, 16).T, (8, 1)).astype(np.uint16)


def unstriped(offs):
    return offs[:16].T.reshape(-1).astype(np.int64)


def striped8(idx):
    return np.concatenate([v.reshape(-1, 16).T for v in idx]).astype(np.uint16)


def unstriped8(offs):
    return np.stack([offs[16 * g:16 * g + 16].T.reshape(-1) for g in range(8)]).astype(np.int64)


E2M1 = np.array([0.0, 0.5, 1.0, 1.5, 2.0, 3.0, 4.0, 6.0, -0.0, -0.5, -1.0, -1.5, -2.0, -3.0, -4.0, -6.0])


def pack_weight(w, fmt):
    k, n = w.shape
    w = f64(np.asarray(w, np.float32).astype(ml_dtypes.bfloat16)).reshape(k // 32, 32, n)
    amax = np.abs(w).max(1)
    if fmt == "e4m3":
        byte = np.frexp(amax)[1] - 1 + 127 - 7
    else:
        mant, ex = np.frexp(amax / 6.0)
        byte = np.where(mant > 0.5, ex, ex - 1) + 127
    byte = np.clip(np.where(amax > 0, byte, 1), 1, 254)
    scaled = (w * np.exp2(127.0 - byte)[:, None, :]).reshape(k, n).astype(np.float32)
    by_word = np.ascontiguousarray(scaled.reshape(k // 512, 128, 4, n).transpose(0, 1, 3, 2))
    if fmt == "e4m3":
        words = by_word.astype(ml_dtypes.float8_e4m3fn).view(np.uint8)
    else:
        c = by_word.astype(ml_dtypes.float4_e2m1fn).view(np.uint8) & 0xF
        words = (c[..., 0::2] | (c[..., 1::2] << 4)).reshape(k // 512, 128, 2 * n)
    return np.ascontiguousarray(words), np.ascontiguousarray(byte.astype(np.uint8).reshape(k // 512, 16, n))


def unpack_weight(words, scales, fmt):
    g, _, n = scales.shape
    words = np.ascontiguousarray(words).reshape(g, 128, n, -1)
    if fmt == "e4m3":
        vals = words.view(ml_dtypes.float8_e4m3fn).astype(np.float64)
    else:
        nib = np.empty((g, 128, n, 4), np.uint8)
        nib[..., 0::2] = words & 0xF
        nib[..., 1::2] = words >> 4
        vals = E2M1[nib]
    vals = vals * np.repeat(np.exp2(scales.astype(np.float64) - 127.0), 8, axis=1)[..., None]
    return vals.transpose(0, 1, 3, 2).reshape(g * 512, n)


def pack_table(v):
    words, scales = pack_weight(v, "e4m3")
    return np.concatenate([words.reshape(words.shape[0], -1), scales.reshape(scales.shape[0], -1)], axis=1)


def unpack_table(tab):
    g, t = tab.shape[0], tab.shape[1] // 528
    return unpack_weight(tab[:, :512 * t].reshape(g, 128, t, 4), tab[:, 512 * t:].reshape(g, 16, t), "e4m3")


K, L, M, T, S = 1024, 512, 128, 2048, 1024


def setup_inputs():
    n = np.random.standard_normal
    s1 = mx_kscale(K)[:, None]
    s2 = mx_kscale(L)[:, None]
    p_w4 = pack_weight(n((K, M)) / np.sqrt(K) / s1, "e2m1")
    return {
        "xT": (n((K, T)) * s1).astype(np.float32),
        "w4_words": p_w4[0],
        "w4_scales": p_w4[1],
        "tab": pack_table(n((L, T)) * s2),
        "u": (n((L, M)) / np.sqrt(L) / s2).astype(np.float32),
        "wgt": np.repeat(np.random.uniform(0.5, 2.0, (8, S)), 16, axis=0).astype(np.float32),
        "b": (0.3 * n(128)).astype(np.float32),
        "offs": striped(np.random.permutation(T)[:S]),
        "offs2": striped8(np.stack([np.random.permutation(T)[:S] for _ in range(8)])),
    }


def reference(xT, w4_words, w4_scales, tab, u, wgt, b, offs, offs2):
    idx2 = unstriped8(offs2)
    group = np.arange(K) % 512 // 64
    xg = f64(wgt)[np.arange(K) // 4 % 128] * f64(xT)[np.arange(K)[:, None], idx2[group]]
    xT_ = mxq(xg, 0, "e4m3")
    w4_ = unpack_weight(w4_words, w4_scales, "e2m1")
    tab_ = unpack_table(tab)[:, unstriped(offs)]
    u_ = mxq(f64(u), 0, "e4m3")
    y = w4_.T @ xT_ + u_.T @ tab_
    return y + f64(b)[:, None]

@@ -1,0 +1,156 @@
+from contextlib import ExitStack
+
+import concourse.mybir as mybir
+
+K, L, M, T, S = 1024, 512, 128, 2048, 1024
+FLOPS = 2 * M * S * (K + L)
+
+F32 = mybir.dt.float32
+BF16 = mybir.dt.bfloat16
+I32 = mybir.dt.int32
+U32 = mybir.dt.uint32
+U16 = mybir.dt.uint16
+U8 = mybir.dt.uint8
+FP8X4 = mybir.dt.float8_e4m3fn_x4
+FP4X4 = mybir.dt.float4_e2m1fn_x4
+MULT = mybir.AluOpType.mult
+ADD = mybir.AluOpType.add
+IDENTITY = mybir.ActivationFunctionType.Identity
+
+P = 128
+PACK = 4
+PASSES = K // (P * PACK)
+GROUP = 16
+HALF = S // 2
+
+
+def tile_list_htab_bias_kernel(tc, xT, w4_words, w4_scales, tab, u, wgt, b, offs, offs2, out):
+    nc = tc.nc
+    with ExitStack() as ctx:
+        keep = ctx.enter_context(tc.tile_pool(name="keep", bufs=1))
+        psum = ctx.enter_context(tc.psum_pool(name="psum", bufs=1))
+
+        tab_list = keep.tile([P, S // GROUP], U16, name="tab_list")
+        head_lists = keep.tile([P, S // GROUP], U16, name="head_lists")
+        nc.sync.dma_start(tab_list[:], offs)
+        nc.sync.dma_start(head_lists[:], offs2)
+
+        tab_scales = keep.tile([P, T], U8, name="tab_scales", align_bytes=64)
+        nc.vector.memset(tab_scales[:].bitcast(I32), 0)
+        w4_plane = keep.tile([P, PASSES, M], U8, name="w4_plane", align_bytes=64)
+        nc.vector.memset(w4_plane[:].bitcast(I32), 0)
+        tab_scale_rows = tab[0, 512 * T : 528 * T].rearrange("(q t) -> q t", q=16).bitcast(I32)
+        for q in range(4):
+            nc.scalar.dma_start(tab_scales[32 * q : 32 * q + 4, :].bitcast(I32), tab_scale_rows[4 * q : 4 * q + 4, :])
+
+        x_rows = xT.rearrange("(a p i) t -> a i p t", a=PASSES, p=P, i=PACK)
+        weights = []
+        planes = {}
+        for h in range(2):
+            wt = keep.tile([P, HALF], F32, name="wgt%d" % h)
+            nc.sync.dma_start(wt[:], wgt[:, h * HALF : (h + 1) * HALF])
+            weights.append(wt)
+            pl = keep.tile([P, T], F32, name="plane0%d" % h)
+            nc.sync.dma_start(pl[:], x_rows[0, h])
+            planes[(0, h)] = pl
+        for a in range(PASSES):
+            for i in range(PACK):
+                if (a, i) not in planes:
+                    pl = keep.tile([P, T], F32, name="plane%d%d" % (a, i))
+                    nc.sync.dma_start(pl[:], x_rows[a, i])
+                    planes[(a, i)] = pl
+        tab_words = keep.tile([P, T], I32, name="tab_words")
+        nc.sync.dma_start(tab_words[:], tab[0, 0 : 512 * T].rearrange("(p c) -> p c", p=P).bitcast(I32))
+
+        u_raw = keep.tile([P, PACK, M], F32, name="u_raw")
+        nc.scalar.dma_start(u_raw[:], u.rearrange("(p i) n -> p i n", i=PACK))
+        w4_codes = keep.tile([P, PASSES, 2 * M], U8, name="w4_codes", align_bytes=64)
+        nc.scalar.dma_start(w4_codes[:].bitcast(I32), w4_words.rearrange("a p c -> p a c").bitcast(I32))
+        for q in range(4):
+            nc.scalar.dma_start(
+                w4_plane[32 * q : 32 * q + 4, :, :].bitcast(I32),
+                w4_scales[:, 4 * q : 4 * q + 4, :].rearrange("a r n -> r a n").bitcast(I32),
+            )
+        bias = keep.tile([P, 1], F32, name="bias")
+        nc.scalar.dma_start(bias[:], b.rearrange("(p o) -> p o", o=1))
+
+        picked_scales = keep.tile([P, S], U8, name="picked_scales", align_bytes=64)
+        nc.vector.tensor_copy(picked_scales[:], tab_scales[:].indirect(tab_list[:]))
+
+        u_grouped = keep.tile([P, M, PACK], BF16, name="u_grouped", align_bytes=64)
+        nc.scalar.copy(u_grouped[:], u_raw[:].rearrange("p i n -> p n i"))
+        u_codes = keep.tile([P, M], U32, name="u_codes", align_bytes=64)
+        u_plane = keep.tile([P, M], U8, name="u_plane", align_bytes=64)
+        nc.vector.quantize_mx(out=u_codes[:].bitcast(FP8X4), scales=u_plane[:], in_=u_grouped[:].rearrange("p n i -> p (n i)"))
+
+        def gather_x(a, i, j0, j1, picked):
+            h = j0 // HALF
+            nc.vector.tensor_tensor(
+                picked[:, i, :],
+                planes[(a, i)][:].indirect(head_lists[:, j0 // GROUP : j1 // GROUP]),
+                weights[h][:, j0 - h * HALF : j1 - h * HALF],
+                MULT,
+            )
+
+        def interleave(a, j0, j1, picked):
+            grouped = keep.tile([P, j1 - j0, PACK], BF16, name="grouped%d_%d" % (a, j0), align_bytes=64)
+            nc.scalar.copy(
+                grouped[:].rearrange("p (c e) i -> p c i e", e=4),
+                picked[:].rearrange("p i (c e) -> p c i e", e=4),
+            )
+            return grouped
+
+        def quantise(a, j0, j1, grouped):
+            codes = keep.tile([P, j1 - j0], U32, name="codes%d_%d" % (a, j0), align_bytes=64)
+            plane = keep.tile([P, j1 - j0], U8, name="scales%d_%d" % (a, j0), align_bytes=64)
+            nc.vector.quantize_mx(out=codes[:].bitcast(FP8X4), scales=plane[:], in_=grouped[:].rearrange("p c i -> p (c i)"))
+            return codes, plane
+
+        halves = [(0, HALF), (HALF, S)]
+        first = [keep.tile([P, PACK, HALF], F32, name="picked0_%d" % h) for h in range(2)]
+        for i in range(PACK):
+            for h in range(2):
+                gather_x(0, i, halves[h][0], halves[h][1], first[h])
+        first_grouped = [interleave(0, halves[h][0], halves[h][1], first[h]) for h in range(2)]
+
+        chunks = [(0, 512), (512, 768), (768, 896), (896, 1024)]
+        banks = [psum.tile([P, j1 - j0], F32, name="bank%d" % j0) for j0, j1 in chunks]
+        second = [keep.tile([P, PACK, j1 - j0], F32, name="picked1_%d" % j0) for j0, j1 in chunks]
+        first_q = []
+        pending = []
+
+        def finish(n, grouped):
+            j0, j1 = chunks[n]
+            codes, plane = quantise(1, j0, j1, grouped)
+            nc.tensor.matmul_mx(
+                out=banks[n][:], lhsT=w4_codes[:, 1, :].bitcast(FP4X4), lhsT_scale=w4_plane[:, 1, :],
+                rhs=codes[:].bitcast(FP8X4), rhs_scale=plane[:], start=False, stop=True,
+            )
+            result = keep.tile([P, j1 - j0], F32, name="result%d" % j0)
+            nc.scalar.activation(result[:], banks[n][:], IDENTITY, bias=bias[:])
+            nc.sync.dma_start(out[:, j0:j1], result[:])
+
+        for n in range(len(chunks)):
+            j0, j1 = chunks[n]
+            for i in range(PACK):
+                gather_x(1, i, j0, j1, second[n])
+                if n == 0 and i < 2:
+                    first_q.append(quantise(0, halves[i][0], halves[i][1], first_grouped[i]))
+            grouped = interleave(1, j0, j1, second[n])
+            picked_words = keep.tile([P, j1 - j0], U32, name="picked_words%d" % j0, align_bytes=64)
+            nc.vector.tensor_copy(picked_words[:], tab_words[:].bitcast(U32).indirect(tab_list[:, j0 // GROUP : j1 // GROUP]))
+            h = j0 // HALF
+            codes, plane = first_q[h]
+            cols = slice(j0 - h * HALF, j1 - h * HALF)
+            nc.tensor.matmul_mx(
+                out=banks[n][:], lhsT=w4_codes[:, 0, :].bitcast(FP4X4), lhsT_scale=w4_plane[:, 0, :],
+                rhs=codes[:, cols].bitcast(FP8X4), rhs_scale=plane[:, cols], start=True, stop=False,
+            )
+            nc.tensor.matmul_mx(
+                out=banks[n][:], lhsT=u_codes[:].bitcast(FP8X4), lhsT_scale=u_plane[:],
+                rhs=picked_words[:].bitcast(FP8X4), rhs_scale=picked_scales[:, j0:j1], start=False, stop=False,
+            )
+            if pending:
+                finish(*pending.pop())
+            pending.append((n, grouped))
+        finish(*pending.pop())

@@ -14,7 +14,6 @@ U8 = mybir.dt.uint8
 FP8X4 = mybir.dt.float8_e4m3fn_x4
 FP4X4 = mybir.dt.float4_e2m1fn_x4
 MULT = mybir.AluOpType.mult
-ADD = mybir.AluOpType.add
 IDENTITY = mybir.ActivationFunctionType.Identity
 
 P = 128
@@ -22,6 +21,7 @@ PACK = 4
 PASSES = K // (P * PACK)
 GROUP = 16
 HALF = S // 2
+SPLIT = 1920
 
 
 def tile_list_htab_bias_kernel(tc, xT, w4_words, w4_scales, tab, u, wgt, b, offs, offs2, out):
@@ -30,127 +30,130 @@ def tile_list_htab_bias_kernel(tc, xT, w4_words, w4_scales, tab, u, wgt, b, offs
         keep = ctx.enter_context(tc.tile_pool(name="keep", bufs=1))
         psum = ctx.enter_context(tc.psum_pool(name="psum", bufs=1))
 
-        tab_list = keep.tile([P, S // GROUP], U16, name="tab_list")
-        head_lists = keep.tile([P, S // GROUP], U16, name="head_lists")
-        nc.sync.dma_start(tab_list[:], offs)
-        nc.sync.dma_start(head_lists[:], offs2)
-
         tab_scales = keep.tile([P, T], U8, name="tab_scales", align_bytes=64)
         nc.vector.memset(tab_scales[:].bitcast(I32), 0)
         w4_plane = keep.tile([P, PASSES, M], U8, name="w4_plane", align_bytes=64)
         nc.vector.memset(w4_plane[:].bitcast(I32), 0)
+
+        tab_list = keep.tile([P, S // GROUP], U16, name="tab_list")
+        head_lists = keep.tile([P, S // GROUP], U16, name="head_lists")
+        nc.sync.dma_start(tab_list[:], offs)
         tab_scale_rows = tab[0, 512 * T : 528 * T].rearrange("(q t) -> q t", q=16).bitcast(I32)
         for q in range(4):
-            nc.scalar.dma_start(tab_scales[32 * q : 32 * q + 4, :].bitcast(I32), tab_scale_rows[4 * q : 4 * q + 4, :])
+            nc.sync.dma_start(tab_scales[32 * q : 32 * q + 4, :].bitcast(I32), tab_scale_rows[4 * q : 4 * q + 4, :])
+        nc.sync.dma_start(head_lists[:], offs2)
 
         x_rows = xT.rearrange("(a p i) t -> a i p t", a=PASSES, p=P, i=PACK)
-        weights = []
-        planes = {}
-        for h in range(2):
-            wt = keep.tile([P, HALF], F32, name="wgt%d" % h)
-            nc.sync.dma_start(wt[:], wgt[:, h * HALF : (h + 1) * HALF])
-            weights.append(wt)
-            pl = keep.tile([P, T], F32, name="plane0%d" % h)
-            nc.sync.dma_start(pl[:], x_rows[0, h])
-            planes[(0, h)] = pl
-        for a in range(PASSES):
-            for i in range(PACK):
-                if (a, i) not in planes:
-                    pl = keep.tile([P, T], F32, name="plane%d%d" % (a, i))
-                    nc.sync.dma_start(pl[:], x_rows[a, i])
-                    planes[(a, i)] = pl
-        tab_words = keep.tile([P, T], I32, name="tab_words")
-        nc.sync.dma_start(tab_words[:], tab[0, 0 : 512 * T].rearrange("(p c) -> p c", p=P).bitcast(I32))
-
+        weights = keep.tile([P, S], F32, name="weights")
+        planes = [keep.tile([P, T], F32, name="plane%d" % n, tag="plane%d" % n, align_bytes=64) for n in range(PASSES * PACK)]
         u_raw = keep.tile([P, PACK, M], F32, name="u_raw")
-        nc.scalar.dma_start(u_raw[:], u.rearrange("(p i) n -> p i n", i=PACK))
         w4_codes = keep.tile([P, PASSES, 2 * M], U8, name="w4_codes", align_bytes=64)
-        nc.scalar.dma_start(w4_codes[:].bitcast(I32), w4_words.rearrange("a p c -> p a c").bitcast(I32))
+        bias = keep.tile([P, 1], F32, name="bias")
+        tab_words = keep.tile([P, T], I32, name="tab_words")
+
+        def load_plane(n):
+            nc.sync.dma_start(planes[n][:], x_rows[n // PACK, n % PACK])
+
+        nc.sync.dma_start(weights[:, 0:HALF], wgt[:, 0:HALF])
+        load_plane(0)
+        nc.sync.dma_start(weights[:, HALF:S], wgt[:, HALF:S])
+        for n in range(1, 5):
+            load_plane(n)
+        nc.sync.dma_start(w4_codes[:].bitcast(I32), w4_words.rearrange("a p c -> p a c").bitcast(I32))
         for q in range(4):
-            nc.scalar.dma_start(
+            nc.sync.dma_start(
                 w4_plane[32 * q : 32 * q + 4, :, :].bitcast(I32),
                 w4_scales[:, 4 * q : 4 * q + 4, :].rearrange("a r n -> r a n").bitcast(I32),
             )
-        bias = keep.tile([P, 1], F32, name="bias")
-        nc.scalar.dma_start(bias[:], b.rearrange("(p o) -> p o", o=1))
+        load_plane(5)
+        nc.sync.dma_start(u_raw[:], u.rearrange("(p i) n -> p i n", i=PACK))
+        load_plane(6)
+        nc.sync.dma_start(bias[:], b.rearrange("(p o) -> p o", o=1))
+        load_plane(7)
+        nc.sync.dma_start(tab_words[:], tab[0, 0 : 512 * T].rearrange("(p c) -> p c", p=P).bitcast(I32))
 
         picked_scales = keep.tile([P, S], U8, name="picked_scales", align_bytes=64)
         nc.vector.tensor_copy(picked_scales[:], tab_scales[:].indirect(tab_list[:]))
 
-        u_grouped = keep.tile([P, M, PACK], BF16, name="u_grouped", align_bytes=64)
-        nc.scalar.copy(u_grouped[:], u_raw[:].rearrange("p i n -> p n i"))
-        u_codes = keep.tile([P, M], U32, name="u_codes", align_bytes=64)
-        u_plane = keep.tile([P, M], U8, name="u_plane", align_bytes=64)
-        nc.vector.quantize_mx(out=u_codes[:].bitcast(FP8X4), scales=u_plane[:], in_=u_grouped[:].rearrange("p n i -> p (n i)"))
-
-        def gather_x(a, i, j0, j1, picked):
-            h = j0 // HALF
+        def gather_x(n, j0, j1, target):
             nc.vector.tensor_tensor(
-                picked[:, i, :],
-                planes[(a, i)][:].indirect(head_lists[:, j0 // GROUP : j1 // GROUP]),
-                weights[h][:, j0 - h * HALF : j1 - h * HALF],
+                target,
+                planes[n][:].indirect(head_lists[:, j0 // GROUP : j1 // GROUP]),
+                weights[:, j0:j1],
                 MULT,
             )
 
-        def interleave(a, j0, j1, picked):
-            grouped = keep.tile([P, j1 - j0, PACK], BF16, name="grouped%d_%d" % (a, j0), align_bytes=64)
-            nc.scalar.copy(
-                grouped[:].rearrange("p (c e) i -> p c i e", e=4),
-                picked[:].rearrange("p i (c e) -> p c i e", e=4),
-            )
-            return grouped
+        def weave(grouped, picked, pair, j0, j1):
+            rows = slice(2 * pair, 2 * pair + 2)
+            nc.scalar.copy(grouped[:, :, rows], picked[:, rows, j0:j1].rearrange("p i c -> p c i"))
 
-        def quantise(a, j0, j1, grouped):
-            codes = keep.tile([P, j1 - j0], U32, name="codes%d_%d" % (a, j0), align_bytes=64)
-            plane = keep.tile([P, j1 - j0], U8, name="scales%d_%d" % (a, j0), align_bytes=64)
+        def quantise(codes, plane, grouped):
             nc.vector.quantize_mx(out=codes[:].bitcast(FP8X4), scales=plane[:], in_=grouped[:].rearrange("p c i -> p (c i)"))
-            return codes, plane
 
         halves = [(0, HALF), (HALF, S)]
-        first = [keep.tile([P, PACK, HALF], F32, name="picked0_%d" % h) for h in range(2)]
-        for i in range(PACK):
-            for h in range(2):
-                gather_x(0, i, halves[h][0], halves[h][1], first[h])
-        first_grouped = [interleave(0, halves[h][0], halves[h][1], first[h]) for h in range(2)]
+        first = keep.tile([P, PACK, S], F32, name="picked0")
+        first_grouped = keep.tile([P, S, PACK], BF16, name="grouped0", align_bytes=64)
+        for j0, j1 in halves:
+            gather_x(0, j0, j1, first[:, 0, j0:j1])
+        for i in range(1, PACK):
+            gather_x(i, 0, S, first[:, i, :])
+            if i % 2:
+                weave(first_grouped, first, i // 2, 0, S)
 
-        chunks = [(0, 512), (512, 768), (768, 896), (896, 1024)]
+        second = keep.tile([P, PACK, S], F32, name="picked1")
+        second_grouped = [
+            keep.tile([P, HALF, PACK], BF16, name="grouped1_%d" % h, tag="grouped1_%d" % h, align_bytes=64) for h in range(2)
+        ]
+        for i in range(2):
+            gather_x(PACK + i, 0, S, second[:, i, :])
+
+        u_grouped = keep.tile([P, M, PACK], BF16, name="u_grouped", align_bytes=64)
+        nc.scalar.copy(u_grouped[:], u_raw[:].rearrange("p i n -> p n i"))
+        for h in range(2):
+            weave(second_grouped[h], second, 0, halves[h][0], halves[h][1])
+        u_codes = keep.tile([P, M], U32, name="u_codes", align_bytes=64)
+        u_plane = keep.tile([P, M], U8, name="u_plane", align_bytes=64)
+
+        chunks = [(0, 512), (512, 768), (768, 1024)]
         banks = [psum.tile([P, j1 - j0], F32, name="bank%d" % j0) for j0, j1 in chunks]
-        second = [keep.tile([P, PACK, j1 - j0], F32, name="picked1_%d" % j0) for j0, j1 in chunks]
-        first_q = []
-        pending = []
 
-        def finish(n, grouped):
+        def multiply_heads(a, n, codes, plane, base):
             j0, j1 = chunks[n]
-            codes, plane = quantise(1, j0, j1, grouped)
             nc.tensor.matmul_mx(
-                out=banks[n][:], lhsT=w4_codes[:, 1, :].bitcast(FP4X4), lhsT_scale=w4_plane[:, 1, :],
-                rhs=codes[:].bitcast(FP8X4), rhs_scale=plane[:], start=False, stop=True,
+                out=banks[n][:], lhsT=w4_codes[:, a, :].bitcast(FP4X4), lhsT_scale=w4_plane[:, a, :],
+                rhs=codes[:, j0 - base : j1 - base].bitcast(FP8X4), rhs_scale=plane[:, j0 - base : j1 - base],
+                start=(a == 0), stop=False,
             )
-            result = keep.tile([P, j1 - j0], F32, name="result%d" % j0)
-            nc.scalar.activation(result[:], banks[n][:], IDENTITY, bias=bias[:])
-            nc.sync.dma_start(out[:, j0:j1], result[:])
 
+        gather_x(PACK + 2, 0, S, second[:, 2, :])
+        quantise(u_codes, u_plane, u_grouped)
+        for h in range(2):
+            j0, j1 = halves[h]
+            gather_x(PACK + 3, j0, j1, second[:, 3, j0:j1])
+            weave(second_grouped[h], second, 1, j0, j1)
+
+        first_codes = keep.tile([P, S], U32, name="codes0", tag="plane7", align_bytes=64)
+        first_plane = keep.tile([P, S], U8, name="scales0", align_bytes=64)
+        quantise(first_codes, first_plane, first_grouped)
         for n in range(len(chunks)):
-            j0, j1 = chunks[n]
-            for i in range(PACK):
-                gather_x(1, i, j0, j1, second[n])
-                if n == 0 and i < 2:
-                    first_q.append(quantise(0, halves[i][0], halves[i][1], first_grouped[i]))
-            grouped = interleave(1, j0, j1, second[n])
-            picked_words = keep.tile([P, j1 - j0], U32, name="picked_words%d" % j0, align_bytes=64)
-            nc.vector.tensor_copy(picked_words[:], tab_words[:].bitcast(U32).indirect(tab_list[:, j0 // GROUP : j1 // GROUP]))
-            h = j0 // HALF
-            codes, plane = first_q[h]
-            cols = slice(j0 - h * HALF, j1 - h * HALF)
-            nc.tensor.matmul_mx(
-                out=banks[n][:], lhsT=w4_codes[:, 0, :].bitcast(FP4X4), lhsT_scale=w4_plane[:, 0, :],
-                rhs=codes[:, cols].bitcast(FP8X4), rhs_scale=plane[:, cols], start=True, stop=False,
-            )
-            nc.tensor.matmul_mx(
-                out=banks[n][:], lhsT=u_codes[:].bitcast(FP8X4), lhsT_scale=u_plane[:],
-                rhs=picked_words[:].bitcast(FP8X4), rhs_scale=picked_scales[:, j0:j1], start=False, stop=False,
-            )
-            if pending:
-                finish(*pending.pop())
-            pending.append((n, grouped))
-        finish(*pending.pop())
+            multiply_heads(0, n, first_codes, first_plane, 0)
+
+        for h in range(2):
+            codes = keep.tile([P, HALF], U32, name="codes1_%d" % h, align_bytes=64)
+            plane = keep.tile([P, HALF], U8, name="scales1_%d" % h, align_bytes=64)
+            quantise(codes, plane, second_grouped[h])
+            mine = [n for n in range(len(chunks)) if chunks[n][0] // HALF == h]
+            for n in mine:
+                multiply_heads(1, n, codes, plane, h * HALF)
+            picked_words = keep.tile([P, HALF], U32, name="picked_words%d" % h, tag="grouped1_%d" % h, align_bytes=64)
+            for n in mine:
+                j0, j1 = chunks[n]
+                cols = slice(j0 - h * HALF, j1 - h * HALF)
+                nc.vector.tensor_copy(picked_words[:, cols], tab_words[:].bitcast(U32).indirect(tab_list[:, j0 // GROUP : j1 // GROUP]))
+                nc.tensor.matmul_mx(
+                    out=banks[n][:], lhsT=u_codes[:].bitcast(FP8X4), lhsT_scale=u_plane[:],
+                    rhs=picked_words[:, cols].bitcast(FP8X4), rhs_scale=picked_scales[:, j0:j1], start=False, stop=True,
+                )
+                result = keep.tile([P, j1 - j0], F32, name="result%d" % j0)
+                nc.scalar.activation(result[:], banks[n][:], IDENTITY, bias=bias[:])
+                nc.sync.dma_start(out[:, j0:j1], result[:])

@@ -1,6 +1,7 @@
 from contextlib import ExitStack
 
 import concourse.mybir as mybir
+from concourse.masks import make_identity
 
 K, L, M, T, S = 1024, 512, 128, 2048, 1024
 FLOPS = 2 * M * S * (K + L)
@@ -38,6 +39,11 @@ def tile_list_htab_bias_kernel(tc, xT, w4_words, w4_scales, tab, u, wgt, b, offs
         tab_list = keep.tile([P, S // GROUP], U16, name="tab_list")
         head_lists = keep.tile([P, S // GROUP], U16, name="head_lists")
         nc.sync.dma_start(tab_list[:], offs)
+        wgt_rows = keep.tile([P, P], F32, name="wgt_rows")
+        nc.gpsimd.memset(wgt_rows[64:128, :], 0.0)
+        nc.sync.dma_start(wgt_rows[0:64, :], wgt.rearrange("(g r) (c j) -> r g c j", r=GROUP, j=P)[0])
+        identity = keep.tile([P, P], F32, name="identity")
+        make_identity(nc, identity[:])
         tab_scale_rows = tab[0, 512 * T : 528 * T].rearrange("(q t) -> q t", q=16).bitcast(I32)
         for q in range(4):
             nc.sync.dma_start(tab_scales[32 * q : 32 * q + 4, :].bitcast(I32), tab_scale_rows[4 * q : 4 * q + 4, :])
@@ -54,23 +60,28 @@ def tile_list_htab_bias_kernel(tc, xT, w4_words, w4_scales, tab, u, wgt, b, offs
         def load_plane(n):
             nc.sync.dma_start(planes[n][:], x_rows[n // PACK, n % PACK])
 
-        nc.sync.dma_start(weights[:, 0:HALF], wgt[:, 0:HALF])
-        load_plane(0)
-        nc.sync.dma_start(weights[:, HALF:S], wgt[:, HALF:S])
-        for n in range(1, 5):
+        for n in range(PASSES * PACK):
             load_plane(n)
+        nc.sync.dma_start(u_raw[:], u.rearrange("(p i) n -> p i n", i=PACK))
+        nc.sync.dma_start(tab_words[:], tab[0, 0 : 512 * T].rearrange("(p c) -> p c", p=P).bitcast(I32))
         nc.sync.dma_start(w4_codes[:].bitcast(I32), w4_words.rearrange("a p c -> p a c").bitcast(I32))
         for q in range(4):
             nc.sync.dma_start(
                 w4_plane[32 * q : 32 * q + 4, :, :].bitcast(I32),
                 w4_scales[:, 4 * q : 4 * q + 4, :].rearrange("a r n -> r a n").bitcast(I32),
             )
-        load_plane(5)
-        nc.sync.dma_start(u_raw[:], u.rearrange("(p i) n -> p i n", i=PACK))
-        load_plane(6)
         nc.sync.dma_start(bias[:], b.rearrange("(p o) -> p o", o=1))
-        load_plane(7)
-        nc.sync.dma_start(tab_words[:], tab[0, 0 : 512 * T].rearrange("(p c) -> p c", p=P).bitcast(I32))
+
+        turned = psum.tile([P, P], F32, name="turned")
+        nc.tensor.transpose(turned[:], wgt_rows[:], identity[:])
+        by_block = turned[:, 0:64].rearrange("j (g c) -> j c g", g=8)
+        for h in range(2):
+            spread = keep.tile([P, 4, 8, GROUP], F32, name="spread%d" % h)
+            nc.scalar.copy(spread[:], by_block[:, 4 * h : 4 * h + 4, :].unsqueeze(3).to_broadcast([P, 4, 8, GROUP]))
+            back = psum.tile([P, HALF], F32, name="back%d" % h)
+            for c in range(4):
+                nc.tensor.transpose(back[:, c * P : (c + 1) * P], spread[:, c, :, :].rearrange("j g r -> j (g r)"), identity[:])
+            nc.scalar.copy(weights[:, h * HALF : (h + 1) * HALF], back[:])
 
         picked_scales = keep.tile([P, S], U8, name="picked_scales", align_bytes=64)
         nc.vector.tensor_copy(picked_scales[:], tab_scales[:].indirect(tab_list[:]))
@@ -88,7 +99,7 @@ def tile_list_htab_bias_kernel(tc, xT, w4_words, w4_scales, tab, u, wgt, b, offs
             nc.scalar.copy(grouped[:, :, rows], picked[:, rows, j0:j1].rearrange("p i c -> p c i"))
 
         def quantise(codes, plane, grouped):
-            nc.vector.quantize_mx(out=codes[:].bitcast(FP8X4), scales=plane[:], in_=grouped[:].rearrange("p c i -> p (c i)"))
+            nc.vector.quantize_mx(out=codes[:].bitcast(FP8X4), scales=plane[:], in_=grouped.rearrange("p c i -> p (c i)"))
 
         halves = [(0, HALF), (HALF, S)]
         first = keep.tile([P, PACK, S], F32, name="picked0")
@@ -108,13 +119,13 @@ def tile_list_htab_bias_kernel(tc, xT, w4_words, w4_scales, tab, u, wgt, b, offs
             gather_x(PACK + i, 0, S, second[:, i, :])
 
         u_grouped = keep.tile([P, M, PACK], BF16, name="u_grouped", align_bytes=64)
-        nc.scalar.copy(u_grouped[:], u_raw[:].rearrange("p i n -> p n i"))
         for h in range(2):
             weave(second_grouped[h], second, 0, halves[h][0], halves[h][1])
+        nc.scalar.copy(u_grouped[:], u_raw[:].rearrange("p i n -> p n i"))
         u_codes = keep.tile([P, M], U32, name="u_codes", align_bytes=64)
         u_plane = keep.tile([P, M], U8, name="u_plane", align_bytes=64)
 
-        chunks = [(0, 512), (512, 768), (768, 1024)]
+        chunks = [(0, 512), (512, 768), (768, 896), (896, 1024)]
         banks = [psum.tile([P, j1 - j0], F32, name="bank%d" % j0) for j0, j1 in chunks]
 
         def multiply_heads(a, n, codes, plane, base):
@@ -125,23 +136,29 @@ def tile_list_htab_bias_kernel(tc, xT, w4_words, w4_scales, tab, u, wgt, b, offs
                 start=(a == 0), stop=False,
             )
 
+        def quantise_first(h):
+            codes = keep.tile([P, HALF], U32, name="codes0_%d" % h, tag="plane%d" % (6 + h), align_bytes=64)
+            plane = keep.tile([P, HALF], U8, name="scales0_%d" % h, align_bytes=64)
+            quantise(codes, plane, first_grouped[:, h * HALF : (h + 1) * HALF, :])
+            return codes, plane
+
         gather_x(PACK + 2, 0, S, second[:, 2, :])
-        quantise(u_codes, u_plane, u_grouped)
+        first_q = [quantise_first(0)]
         for h in range(2):
             j0, j1 = halves[h]
             gather_x(PACK + 3, j0, j1, second[:, 3, j0:j1])
             weave(second_grouped[h], second, 1, j0, j1)
 
-        first_codes = keep.tile([P, S], U32, name="codes0", tag="plane7", align_bytes=64)
-        first_plane = keep.tile([P, S], U8, name="scales0", align_bytes=64)
-        quantise(first_codes, first_plane, first_grouped)
+        first_q.append(quantise_first(1))
+        quantise(u_codes, u_plane, u_grouped[:])
         for n in range(len(chunks)):
-            multiply_heads(0, n, first_codes, first_plane, 0)
+            h = chunks[n][0] // HALF
+            multiply_heads(0, n, first_q[h][0], first_q[h][1], h * HALF)
 
         for h in range(2):
             codes = keep.tile([P, HALF], U32, name="codes1_%d" % h, align_bytes=64)
             plane = keep.tile([P, HALF], U8, name="scales1_%d" % h, align_bytes=64)
-            quantise(codes, plane, second_grouped[h])
+            quantise(codes, plane, second_grouped[h][:])
             mine = [n for n in range(len(chunks)) if chunks[n][0] // HALF == h]
             for n in mine:
                 multiply_heads(1, n, codes, plane, h * HALF)

@@ -38,10 +38,10 @@ def tile_list_htab_bias_kernel(tc, xT, w4_words, w4_scales, tab, u, wgt, b, offs
 
         tab_list = keep.tile([P, S // GROUP], U16, name="tab_list")
         head_lists = keep.tile([P, S // GROUP], U16, name="head_lists")
-        nc.sync.dma_start(tab_list[:], offs)
         wgt_rows = keep.tile([P, P], F32, name="wgt_rows")
         nc.gpsimd.memset(wgt_rows[64:128, :], 0.0)
         nc.sync.dma_start(wgt_rows[0:64, :], wgt.rearrange("(g r) (c j) -> r g c j", r=GROUP, j=P)[0])
+        nc.sync.dma_start(tab_list[:], offs)
         identity = keep.tile([P, P], F32, name="identity")
         make_identity(nc, identity[:])
         tab_scale_rows = tab[0, 512 * T : 528 * T].rearrange("(q t) -> q t", q=16).bitcast(I32)
@@ -75,13 +75,13 @@ def tile_list_htab_bias_kernel(tc, xT, w4_words, w4_scales, tab, u, wgt, b, offs
         turned = psum.tile([P, P], F32, name="turned")
         nc.tensor.transpose(turned[:], wgt_rows[:], identity[:])
         by_block = turned[:, 0:64].rearrange("j (g c) -> j c g", g=8)
-        for h in range(2):
-            spread = keep.tile([P, 4, 8, GROUP], F32, name="spread%d" % h)
-            nc.scalar.copy(spread[:], by_block[:, 4 * h : 4 * h + 4, :].unsqueeze(3).to_broadcast([P, 4, 8, GROUP]))
-            back = psum.tile([P, HALF], F32, name="back%d" % h)
-            for c in range(4):
+        for n in range(4):
+            spread = keep.tile([P, 2, 8, GROUP], F32, name="spread%d" % n)
+            nc.scalar.copy(spread[:], by_block[:, 2 * n : 2 * n + 2, :].unsqueeze(3).to_broadcast([P, 2, 8, GROUP]))
+            back = psum.tile([P, 2 * P], F32, name="back%d" % n, tag="bank%d" % n)
+            for c in range(2):
                 nc.tensor.transpose(back[:, c * P : (c + 1) * P], spread[:, c, :, :].rearrange("j g r -> j (g r)"), identity[:])
-            nc.scalar.copy(weights[:, h * HALF : (h + 1) * HALF], back[:])
+            nc.scalar.copy(weights[:, 2 * n * P : 2 * (n + 1) * P], back[:])
 
         picked_scales = keep.tile([P, S], U8, name="picked_scales", align_bytes=64)
         nc.vector.tensor_copy(picked_scales[:], tab_scales[:].indirect(tab_list[:]))
@@ -126,7 +126,7 @@ def tile_list_htab_bias_kernel(tc, xT, w4_words, w4_scales, tab, u, wgt, b, offs
         u_plane = keep.tile([P, M], U8, name="u_plane", align_bytes=64)
 
         chunks = [(0, 512), (512, 768), (768, 896), (896, 1024)]
-        banks = [psum.tile([P, j1 - j0], F32, name="bank%d" % j0) for j0, j1 in chunks]
+        banks = [psum.tile([P, chunks[n][1] - chunks[n][0]], F32, name="bank%d" % n, tag="bank%d" % n) for n in range(len(chunks))]
 
         def multiply_heads(a, n, codes, plane, base):
             j0, j1 = chunks[n]
@@ -136,24 +136,18 @@ def tile_list_htab_bias_kernel(tc, xT, w4_words, w4_scales, tab, u, wgt, b, offs
                 start=(a == 0), stop=False,
             )
 
-        def quantise_first(h):
-            codes = keep.tile([P, HALF], U32, name="codes0_%d" % h, tag="plane%d" % (6 + h), align_bytes=64)
-            plane = keep.tile([P, HALF], U8, name="scales0_%d" % h, align_bytes=64)
-            quantise(codes, plane, first_grouped[:, h * HALF : (h + 1) * HALF, :])
-            return codes, plane
-
         gather_x(PACK + 2, 0, S, second[:, 2, :])
-        first_q = [quantise_first(0)]
         for h in range(2):
             j0, j1 = halves[h]
             gather_x(PACK + 3, j0, j1, second[:, 3, j0:j1])
             weave(second_grouped[h], second, 1, j0, j1)
 
-        first_q.append(quantise_first(1))
+        first_codes = keep.tile([P, S], U32, name="codes0", tag="plane7", align_bytes=64)
+        first_plane = keep.tile([P, S], U8, name="scales0", align_bytes=64)
+        quantise(first_codes, first_plane, first_grouped[:])
         quantise(u_codes, u_plane, u_grouped[:])
         for n in range(len(chunks)):
-            h = chunks[n][0] // HALF
-            multiply_heads(0, n, first_q[h][0], first_q[h][1], h * HALF)
+            multiply_heads(0, n, first_codes, first_plane, 0)
 
         for h in range(2):
             codes = keep.tile([P, HALF], U32, name="codes1_%d" % h, align_bytes=64)
@@ -162,7 +156,7 @@ def tile_list_htab_bias_kernel(tc, xT, w4_words, w4_scales, tab, u, wgt, b, offs
             mine = [n for n in range(len(chunks)) if chunks[n][0] // HALF == h]
             for n in mine:
                 multiply_heads(1, n, codes, plane, h * HALF)
-            picked_words = keep.tile([P, HALF], U32, name="picked_words%d" % h, tag="grouped1_%d" % h, align_bytes=64)
+            picked_words = keep.tile([P, HALF], U32, name="picked_words%d" % h, tag=("picked_words0", "grouped1_1")[h], align_bytes=64)
             for n in mine:
                 j0, j1 = chunks[n]
                 cols = slice(j0 - h * HALF, j1 - h * HALF)

from contextlib import ExitStack

import concourse.mybir as mybir
from concourse.masks import make_identity

K, L, M, T, S = 1024, 512, 128, 2048, 1024
FLOPS = 2 * M * S * (K + L)

F32 = mybir.dt.float32
BF16 = mybir.dt.bfloat16
I32 = mybir.dt.int32
U32 = mybir.dt.uint32
U16 = mybir.dt.uint16
U8 = mybir.dt.uint8
FP8X4 = mybir.dt.float8_e4m3fn_x4
FP4X4 = mybir.dt.float4_e2m1fn_x4
MULT = mybir.AluOpType.mult
IDENTITY = mybir.ActivationFunctionType.Identity

P = 128
PACK = 4
PASSES = K // (P * PACK)
GROUP = 16
HALF = S // 2
SPLIT = 1920


def tile_list_htab_bias_kernel(tc, xT, w4_words, w4_scales, tab, u, wgt, b, offs, offs2, out):
    nc = tc.nc
    with ExitStack() as ctx:
        keep = ctx.enter_context(tc.tile_pool(name="keep", bufs=1))
        psum = ctx.enter_context(tc.psum_pool(name="psum", bufs=1))

        tab_scales = keep.tile([P, T], U8, name="tab_scales", align_bytes=64)
        nc.vector.memset(tab_scales[:].bitcast(I32), 0)
        w4_plane = keep.tile([P, PASSES, M], U8, name="w4_plane", align_bytes=64)
        nc.vector.memset(w4_plane[:].bitcast(I32), 0)

        tab_list = keep.tile([P, S // GROUP], U16, name="tab_list")
        head_lists = keep.tile([P, S // GROUP], U16, name="head_lists")
        wgt_rows = keep.tile([P, P], F32, name="wgt_rows")
        nc.gpsimd.memset(wgt_rows[64:128, :], 0.0)
        nc.sync.dma_start(wgt_rows[0:64, :], wgt.rearrange("(g r) (c j) -> r g c j", r=GROUP, j=P)[0])
        nc.sync.dma_start(tab_list[:], offs)
        identity = keep.tile([P, P], F32, name="identity")
        make_identity(nc, identity[:])
        tab_scale_rows = tab[0, 512 * T : 528 * T].rearrange("(q t) -> q t", q=16).bitcast(I32)
        for q in range(4):
            nc.sync.dma_start(tab_scales[32 * q : 32 * q + 4, :].bitcast(I32), tab_scale_rows[4 * q : 4 * q + 4, :])
        nc.sync.dma_start(head_lists[:], offs2)

        x_rows = xT.rearrange("(a p i) t -> a i p t", a=PASSES, p=P, i=PACK)
        weights = keep.tile([P, S], F32, name="weights")
        planes = [keep.tile([P, T], F32, name="plane%d" % n, tag="plane%d" % n, align_bytes=64) for n in range(PASSES * PACK)]
        u_raw = keep.tile([P, PACK, M], F32, name="u_raw")
        w4_codes = keep.tile([P, PASSES, 2 * M], U8, name="w4_codes", align_bytes=64)
        bias = keep.tile([P, 1], F32, name="bias")
        tab_words = keep.tile([P, T], I32, name="tab_words")

        def load_plane(n):
            nc.sync.dma_start(planes[n][:], x_rows[n // PACK, n % PACK])

        for n in range(PASSES * PACK):
            load_plane(n)
        nc.sync.dma_start(u_raw[:], u.rearrange("(p i) n -> p i n", i=PACK))
        nc.sync.dma_start(tab_words[:], tab[0, 0 : 512 * T].rearrange("(p c) -> p c", p=P).bitcast(I32))
        nc.sync.dma_start(w4_codes[:].bitcast(I32), w4_words.rearrange("a p c -> p a c").bitcast(I32))
        for q in range(4):
            nc.sync.dma_start(
                w4_plane[32 * q : 32 * q + 4, :, :].bitcast(I32),
                w4_scales[:, 4 * q : 4 * q + 4, :].rearrange("a r n -> r a n").bitcast(I32),
            )
        nc.sync.dma_start(bias[:], b.rearrange("(p o) -> p o", o=1))

        turned = psum.tile([P, P], F32, name="turned")
        nc.tensor.transpose(turned[:], wgt_rows[:], identity[:])
        by_block = turned[:, 0:64].rearrange("j (g c) -> j c g", g=8)
        for n in range(4):
            spread = keep.tile([P, 2, 8, GROUP], F32, name="spread%d" % n)
            nc.scalar.copy(spread[:], by_block[:, 2 * n : 2 * n + 2, :].unsqueeze(3).to_broadcast([P, 2, 8, GROUP]))
            back = psum.tile([P, 2 * P], F32, name="back%d" % n, tag="bank%d" % n)
            for c in range(2):
                nc.tensor.transpose(back[:, c * P : (c + 1) * P], spread[:, c, :, :].rearrange("j g r -> j (g r)"), identity[:])
            nc.scalar.copy(weights[:, 2 * n * P : 2 * (n + 1) * P], back[:])

        picked_scales = keep.tile([P, S], U8, name="picked_scales", align_bytes=64)
        nc.vector.tensor_copy(picked_scales[:], tab_scales[:].indirect(tab_list[:]))

        def gather_x(n, j0, j1, target):
            nc.vector.tensor_tensor(
                target,
                planes[n][:].indirect(head_lists[:, j0 // GROUP : j1 // GROUP]),
                weights[:, j0:j1],
                MULT,
            )

        def weave(grouped, picked, pair, j0, j1):
            rows = slice(2 * pair, 2 * pair + 2)
            nc.scalar.copy(grouped[:, :, rows], picked[:, rows, j0:j1].rearrange("p i c -> p c i"))

        def quantise(codes, plane, grouped):
            nc.vector.quantize_mx(out=codes[:].bitcast(FP8X4), scales=plane[:], in_=grouped.rearrange("p c i -> p (c i)"))

        halves = [(0, HALF), (HALF, S)]
        first = keep.tile([P, PACK, S], F32, name="picked0")
        first_grouped = keep.tile([P, S, PACK], BF16, name="grouped0", align_bytes=64)
        for j0, j1 in halves:
            gather_x(0, j0, j1, first[:, 0, j0:j1])
        for i in range(1, PACK):
            gather_x(i, 0, S, first[:, i, :])
            if i % 2:
                weave(first_grouped, first, i // 2, 0, S)

        second = keep.tile([P, PACK, S], F32, name="picked1")
        second_grouped = [
            keep.tile([P, HALF, PACK], BF16, name="grouped1_%d" % h, tag="grouped1_%d" % h, align_bytes=64) for h in range(2)
        ]
        for i in range(2):
            gather_x(PACK + i, 0, S, second[:, i, :])

        u_grouped = keep.tile([P, M, PACK], BF16, name="u_grouped", align_bytes=64)
        for h in range(2):
            weave(second_grouped[h], second, 0, halves[h][0], halves[h][1])
        nc.scalar.copy(u_grouped[:], u_raw[:].rearrange("p i n -> p n i"))
        u_codes = keep.tile([P, M], U32, name="u_codes", align_bytes=64)
        u_plane = keep.tile([P, M], U8, name="u_plane", align_bytes=64)

        chunks = [(0, 512), (512, 768), (768, 896), (896, 1024)]
        banks = [psum.tile([P, chunks[n][1] - chunks[n][0]], F32, name="bank%d" % n, tag="bank%d" % n) for n in range(len(chunks))]

        def multiply_heads(a, n, codes, plane, base):
            j0, j1 = chunks[n]
            nc.tensor.matmul_mx(
                out=banks[n][:], lhsT=w4_codes[:, a, :].bitcast(FP4X4), lhsT_scale=w4_plane[:, a, :],
                rhs=codes[:, j0 - base : j1 - base].bitcast(FP8X4), rhs_scale=plane[:, j0 - base : j1 - base],
                start=(a == 0), stop=False,
            )

        gather_x(PACK + 2, 0, S, second[:, 2, :])
        for h in range(2):
            j0, j1 = halves[h]
            gather_x(PACK + 3, j0, j1, second[:, 3, j0:j1])
            weave(second_grouped[h], second, 1, j0, j1)

        first_codes = keep.tile([P, S], U32, name="codes0", tag="plane7", align_bytes=64)
        first_plane = keep.tile([P, S], U8, name="scales0", align_bytes=64)
        quantise(first_codes, first_plane, first_grouped[:])
        quantise(u_codes, u_plane, u_grouped[:])
        for n in range(len(chunks)):
            multiply_heads(0, n, first_codes, first_plane, 0)

        for h in range(2):
            codes = keep.tile([P, HALF], U32, name="codes1_%d" % h, align_bytes=64)
            plane = keep.tile([P, HALF], U8, name="scales1_%d" % h, align_bytes=64)
            quantise(codes, plane, second_grouped[h][:])
            mine = [n for n in range(len(chunks)) if chunks[n][0] // HALF == h]
            for n in mine:
                multiply_heads(1, n, codes, plane, h * HALF)
            picked_words = keep.tile([P, HALF], U32, name="picked_words%d" % h, tag=("picked_words0", "grouped1_1")[h], align_bytes=64)
            for n in mine:
                j0, j1 = chunks[n]
                cols = slice(j0 - h * HALF, j1 - h * HALF)
                nc.vector.tensor_copy(picked_words[:, cols], tab_words[:].bitcast(U32).indirect(tab_list[:, j0 // GROUP : j1 // GROUP]))
                nc.tensor.matmul_mx(
                    out=banks[n][:], lhsT=u_codes[:].bitcast(FP8X4), lhsT_scale=u_plane[:],
                    rhs=picked_words[:, cols].bitcast(FP8X4), rhs_scale=picked_scales[:, j0:j1], start=False, stop=True,
                )
                result = keep.tile([P, j1 - j0], F32, name="result%d" % j0)
                nc.scalar.activation(result[:], banks[n][:], IDENTITY, bias=bias[:])
                nc.sync.dma_start(out[:, j0:j1], result[:])
